import numpy as np
import ml_dtypes


def mxq(x, axis, fmt="e4m3"):
    dtype, down = {"e4m3": (ml_dtypes.float8_e4m3fn, 7), "e5m2": (ml_dtypes.float8_e5m2, 14)}[fmt]
    v = np.moveaxis(np.asarray(x, np.float32).astype(ml_dtypes.bfloat16).astype(np.float64), axis, -1)
    blocks = v.reshape(v.shape[:-1] + (-1, 32))
    amax = np.abs(blocks).max(-1, keepdims=True)
    byte = np.maximum(np.where(amax > 0, np.frexp(amax)[1] - 1 + 127, 0) - down, 1)
    scale = np.exp2(byte - 127.0)
    codes = (blocks / scale).astype(np.float32).astype(dtype).astype(np.float64)
    return np.moveaxis((codes * scale).reshape(v.shape), -1, axis)


WIDE = False


def mx_kscale(k):
    if not WIDE:
        return np.ones(k)
    levels = np.array([30, -30])
    if k % 512:
        return np.exp2(np.random.permutation(np.resize(levels, k // 32))).repeat(32)
    a = np.empty((k // 512, 16))
    for p in range(k // 512):
        a[p, :8] = np.random.permutation(np.resize(levels, 8))
        for g in range(8):
            far = levels[np.abs(levels - a[p, g]) >= 10]
            a[p, g + 8] = far[np.random.randint(len(far))]
    return np.exp2(a.ravel()).repeat(32)


def f64(x):
    return np.asarray(x).astype(np.float64)


def striped(idx):
    return np.tile(np.asarray(idx).reshape(-1, 16).T, (8, 1)).astype(np.uint16)


def unstriped(offs):
    return offs[:16].T.reshape(-1).astype(np.int64)


E2M1 = np.array([0.0, 0.5, 1.0, 1.5, 2.0, 3.0, 4.0, 6.0, -0.0, -0.5, -1.0, -1.5, -2.0, -3.0, -4.0, -6.0])


def pack_weight(w, fmt):
    k, n = w.shape
    w = f64(np.asarray(w, np.float32).astype(ml_dtypes.bfloat16)).reshape(k // 32, 32, n)
    amax = np.abs(w).max(1)
    if fmt in ("e4m3", "e5m2"):
        byte = np.frexp(amax)[1] - 1 + 127 - (7 if fmt == "e4m3" else 14)
    else:
        mant, ex = np.frexp(amax / 6.0)
        byte = np.where(mant > 0.5, ex, ex - 1) + 127
    byte = np.clip(np.where(amax > 0, byte, 1), 1, 254)
    scaled = (w * np.exp2(127.0 - byte)[:, None, :]).reshape(k, n).astype(np.float32)
    by_word = np.ascontiguousarray(scaled.reshape(k // 512, 128, 4, n).transpose(0, 1, 3, 2))
    if fmt in ("e4m3", "e5m2"):
        words = by_word.astype(ml_dtypes.float8_e4m3fn if fmt == "e4m3" else ml_dtypes.float8_e5m2).view(np.uint8)
    else:
        c = by_word.astype(ml_dtypes.float4_e2m1fn).view(np.uint8) & 0xF
        words = (c[..., 0::2] | (c[..., 1::2] << 4)).reshape(k // 512, 128, 2 * n)
    return np.ascontiguousarray(words), np.ascontiguousarray(byte.astype(np.uint8).reshape(k // 512, 16, n))


def unpack_weight(words, scales, fmt):
    g, _, n = scales.shape
    words = np.ascontiguousarray(words).reshape(g, 128, n, -1)
    if fmt in ("e4m3", "e5m2"):
        vals = words.view(ml_dtypes.float8_e4m3fn if fmt == "e4m3" else ml_dtypes.float8_e5m2).astype(np.float64)
    else:
        nib = np.empty((g, 128, n, 4), np.uint8)
        nib[..., 0::2] = words & 0xF
        nib[..., 1::2] = words >> 4
        vals = E2M1[nib]
    vals = vals * np.repeat(np.exp2(scales.astype(np.float64) - 127.0), 8, axis=1)[..., None]
    return vals.transpose(0, 1, 3, 2).reshape(g * 512, n)


def sigmoid(v):
    return 1.0 / (1.0 + np.exp(-v))


K, T, Z, J, R, Q, N, L, E = 512, 1024, 1024, 256, 512, 1024, 256, 512, 1024


def setup_inputs():
    n = np.random.standard_normal
    idx = np.random.permutation(T)[:J]
    idx2 = np.random.permutation(Z)[:J]
    idx3 = np.random.permutation(Q)[:J]
    idx4 = np.random.permutation(E)[:J]
    fk = mx_kscale(K)
    fr = mx_kscale(R)
    fl = mx_kscale(L)
    xtp = pack_weight(n((K, T)) / fk[:, None], "e4m3")
    xop = pack_weight(n((K, Z)) / fk[:, None], "e2m1")
    wp = pack_weight(n((K, R)) * 1 / np.sqrt(K) * fk[:, None] * fr, "e5m2")
    wbp = pack_weight(n((R, N)) * 1 / np.sqrt(R) / fr[:, None], "e5m2")
    sxp = pack_weight(n((L, J)) / fl[:, None], "e2m1")
    wsp = pack_weight(n((L, N)) * 1 / np.sqrt(L) * fl[:, None], "e5m2")
    return {
        "xt_words": xtp[0],
        "xt_scales": xtp[1],
        "xo_words": xop[0],
        "xo_scales": xop[1],
        "w_words": wp[0],
        "w_scales": wp[1],
        "tg": (1.0 * n((R, Q))).astype(np.float32),
        "sg": (np.random.uniform(0.6, 1.6, (R, 1))).astype(np.float32),
        "bg": (np.random.uniform(-1.0, 1.0, (R, 1))).astype(np.float32),
        "wb_words": wbp[0],
        "wb_scales": wbp[1],
        "sx_words": sxp[0],
        "sx_scales": sxp[1],
        "ws_words": wsp[0],
        "ws_scales": wsp[1],
        "offs": striped(idx),
        "offs2": striped(idx2),
        "offs3": striped(idx3),
        "offs4": striped(idx4),
    }


def reference(xt_words, xt_scales, xo_words, xo_scales, w_words, w_scales, tg, sg, bg, wb_words, wb_scales, sx_words, sx_scales, ws_words, ws_scales, offs, offs2, offs3, offs4):
    idx = unstriped(offs)
    idx2 = unstriped(offs2)
    idx3 = unstriped(offs3)
    idx4 = unstriped(offs4)
    xtu = unpack_weight(xt_words, xt_scales, "e4m3")
    xou = unpack_weight(xo_words, xo_scales, "e2m1")
    wu = unpack_weight(w_words, w_scales, "e5m2")
    wbu = unpack_weight(wb_words, wb_scales, "e5m2")
    sxu = unpack_weight(sx_words, sx_scales, "e2m1")
    wsu = unpack_weight(ws_words, ws_scales, "e5m2")
    xtidxg = xtu[:, idx]
    a = wu.T @ xtidxg
    xoidx2g = xou[:, idx2]
    b = wu.T @ xoidx2g
    hid = np.maximum(a, b) * sigmoid(f64(tg)[:, idx3] * f64(sg) + f64(bg))
    hidq = mxq(hid, 0, "e4m3")
    p = wbu.T @ hidq + wsu.T @ sxu
    y = np.zeros((N, E))
    y[:, idx4] = p
    return y

@@ -1,0 +1,190 @@
+from contextlib import ExitStack
+
+import concourse.mybir as mybir
+
+K, T, J, R, N, E = 512, 1024, 256, 512, 256, 1024
+FLOPS = 2 * J * (2 * K * R + 2 * R * N)
+
+F32 = mybir.dt.float32
+BF16 = mybir.dt.bfloat16
+I32 = mybir.dt.int32
+U32 = mybir.dt.uint32
+U16 = mybir.dt.uint16
+U8 = mybir.dt.uint8
+E4M3 = mybir.dt.float8_e4m3fn_x4
+E5M2 = mybir.dt.float8_e5m2_x4
+E2M1 = mybir.dt.float4_e2m1fn_x4
+ALU = mybir.AluOpType
+ACT = mybir.ActivationFunctionType
+AXIS = mybir.AxisListType
+
+P = 128
+PACK = 4
+ROWS = 16
+ROW0 = P - ROWS
+HALF = J // 2
+
+XT_S, XO_S, W_S, WB_S, WS_S, SX_S, S_END = 0, 256, 512, 1024, 1280, 1536, 1792
+WB_W, WS_W, SX_W, W_END = 0, 1024, 2048, 2560
+
+
+def tile_list_oneforboth_tablegate_skip_scattered_kernel(
+    tc, xt_words, xt_scales, xo_words, xo_scales, w_words, w_scales, tg, sg, bg,
+    wb_words, wb_scales, sx_words, sx_scales, ws_words, ws_scales,
+    offs, offs2, offs3, offs4, out,
+):
+    nc = tc.nc
+    with ExitStack() as ctx:
+        sb = ctx.enter_context(tc.tile_pool(name="sb", bufs=1))
+        ps = ctx.enter_context(tc.psum_pool(name="ps", bufs=1))
+
+        def tile(name, width, dtype, tag=""):
+            return sb.tile([P, width], dtype, name=name, tag=tag or name, align_bytes=64)
+
+        def load_list(name, src):
+            dst = sb.tile([P, J // 16], U16, name=name)
+            nc.sync.dma_start(dst[:], src)
+            return dst
+
+        def load_words(dst, src):
+            nc.sync.dma_start(dst.bitcast(I32), src.bitcast(I32))
+
+        def load_scale_rows(dst, src):
+            nc.sync.dma_start(dst.bitcast(I32), src[0].bitcast(I32))
+
+        xt_s_win = tile("xt_s_win", T, U8)
+        xo_s_win = tile("xo_s_win", T, U8)
+        w_s_raw = tile("w_s_raw", R, U8)
+        rows = tile("rows", W_END, U8, tag="rows_then_words")
+        planes = tile("planes", S_END, U8)
+        xt_win = tile("xt_win", T, U32)
+        xo_win = tile("xo_win", T, U16)
+        w_raw = tile("w_raw", R, I32)
+        pages = [tile(f"page{i}", E, F32) for i in range(N // P)]
+
+        list_xt = load_list("list_xt", offs)
+        list_xo = load_list("list_xo", offs2)
+        for dst, src in ((xt_s_win, xt_scales), (xo_s_win, xo_scales), (w_s_raw, w_scales)):
+            nc.vector.memset(dst[0:ROW0, :].bitcast(I32), 0)
+            load_scale_rows(dst[ROW0:P, :], src)
+        load_words(xo_win[:], xo_words[0])
+        load_words(w_raw[:], w_words[0].rearrange("p c r -> p (c r)"))
+        load_words(xt_win[:], xt_words[0].rearrange("p c r -> p (c r)"))
+        for c0, src in ((WB_S, wb_scales), (WS_S, ws_scales), (SX_S, sx_scales)):
+            load_scale_rows(rows[ROW0:P, c0 : c0 + 256], src)
+        list_tg = load_list("list_tg", offs3)
+        list_out = load_list("list_out", offs4)
+        slope = tile("slope", PACK, F32)
+        shift = tile("shift", PACK, F32)
+        nc.gpsimd.dma_start(slope[:], sg.rearrange("(p t) o -> p (t o)", t=PACK))
+        nc.gpsimd.dma_start(shift[:], bg.rearrange("(p t) o -> p (t o)", t=PACK))
+        tg_by_t = tg.rearrange("(p t) q -> p t q", t=PACK)
+        tg_win = [tile(f"tg_win{t}", T, F32) for t in range(PACK)]
+        for t in range(PACK):
+            nc.sync.dma_start(tg_win[t][:], tg_by_t[:, t, :])
+
+        nc.vector.memset(planes[:].bitcast(I32), 0)
+        for page in pages:
+            nc.vector.memset(page[:], 0.0)
+
+        xt_s = tile("xt_s", J, U8)
+        xo_s = tile("xo_s", J, U8)
+        nc.vector.tensor_copy(xt_s[:], xt_s_win[:].indirect(list_xt[:]))
+        nc.vector.tensor_copy(xo_s[:], xo_s_win[:].indirect(list_xo[:]))
+        nc.vector.tensor_copy(
+            rows[:, W_S:WB_S].rearrange("p (t c i) -> p c t i", t=PACK, i=16),
+            w_s_raw[:].rearrange("p (c i t) -> p c t i", t=PACK, i=16),
+        )
+        nc.vector.tensor_copy(rows[:, XT_S:XO_S].bitcast(I32), xt_s[:].bitcast(I32))
+        nc.vector.tensor_copy(rows[:, XO_S:W_S].bitcast(I32), xo_s[:].bitcast(I32))
+        for q in range(4):
+            nc.scalar.dma_start(
+                planes[32 * q : 32 * q + 4, :].bitcast(I32),
+                rows[ROW0 + 4 * q : ROW0 + 4 * q + 4, 0:S_END].bitcast(I32),
+            )
+
+        late = tile("late", W_END, U8, tag="rows_then_words")
+        load_words(late[:, WS_W:SX_W], ws_words[0].rearrange("p c r -> p (c r)"))
+        load_words(late[:, SX_W:W_END], sx_words[0])
+        load_words(late[:, WB_W:WS_W], wb_words[0].rearrange("p c r -> p (c r)"))
+
+        xo_g = tile("xo_g", J, U16)
+        xt_g = tile("xt_g", J, U32)
+        w_dealt = tile("w_dealt", R, I32)
+        nc.vector.tensor_copy(xo_g[:], xo_win[:].indirect(list_xo[:]))
+        nc.vector.tensor_copy(
+            w_dealt[:].rearrange("p (t c i) -> p c t i", t=PACK, i=4),
+            w_raw[:].rearrange("p (c i t) -> p c t i", t=PACK, i=4),
+        )
+        nc.vector.tensor_copy(xt_g[:], xt_win[:].indirect(list_xt[:]))
+
+        hid = tile("hid", PACK * J, BF16)
+        for t in range(PACK):
+            gate = tile(f"gate{t}", J, F32)
+            nc.scalar.activation(
+                out=gate[:], in_=tg_win[t][:].indirect(list_tg[:]), func=ACT.Sigmoid,
+                bias=shift[:, t : t + 1], scale=slope[:, t : t + 1],
+            )
+            ab = ps.tile([P, 2, J], F32, name=f"ab{t}")
+            for side, (codes, c0) in enumerate(((xo_g[:].bitcast(E2M1), XO_S), (xt_g[:].bitcast(E4M3), XT_S))):
+                nc.tensor.matmul_mx(
+                    out=ab[:, side, :],
+                    lhsT=w_dealt[:, t * P : (t + 1) * P].bitcast(E5M2),
+                    lhsT_scale=planes[:, W_S + t * P : W_S + (t + 1) * P],
+                    rhs=codes, rhs_scale=planes[:, c0 : c0 + J],
+                    start=True, stop=True,
+                )
+            larger = tile(f"larger{t}", J, F32)
+            if t < PACK - 1:
+                first = tile(f"first{t}", J, F32)
+                nc.scalar.copy(first[:], ab[:, 0, :])
+                nc.vector.tensor_tensor(larger[:], ab[:, 1, :], first[:], ALU.max)
+            else:
+                nc.vector.tensor_reduce(larger[:], ab[:].rearrange("p s j -> p j s"), AXIS.X, ALU.max)
+            nc.vector.tensor_tensor(hid[:, t * J : (t + 1) * J], larger[:], gate[:], ALU.mult)
+
+        hid_by_t = hid[:].rearrange("p (t j) -> p t j", t=PACK)
+        codes, scales, woven = [], [], []
+        for h in range(2):
+            wv = tile(f"woven{h}", PACK * HALF, BF16)
+            nc.vector.tensor_copy(
+                wv[:].rearrange("p (c i t) -> p c t i", t=PACK, i=4),
+                hid_by_t[:, :, h * HALF : (h + 1) * HALF].rearrange("p t (c i) -> p c t i", i=4),
+            )
+            woven.append(wv)
+        for h in range(2):
+            codes.append(tile(f"hid_codes{h}", HALF, U32))
+            scales.append(tile(f"hid_scales{h}", HALF, U8))
+            nc.vector.quantize_mx(out=codes[h][:].bitcast(E4M3), scales=scales[h][:], in_=woven[h][:])
+
+        for h in range(2):
+            slots = list_out[:, h * HALF // 16 : (h + 1) * HALF // 16]
+            staged = []
+            for i in range(N // P):
+                acc = ps.tile([P, HALF], F32, name=f"acc{h}{i}")
+                nc.tensor.matmul_mx(
+                    out=acc[:],
+                    lhsT=late[:, WS_W + 4 * i * P : WS_W + 4 * (i + 1) * P].bitcast(E5M2),
+                    lhsT_scale=planes[:, WS_S + i * P : WS_S + (i + 1) * P],
+                    rhs=late[:, SX_W + 2 * h * HALF : SX_W + 2 * (h + 1) * HALF].bitcast(E2M1),
+                    rhs_scale=planes[:, SX_S + h * HALF : SX_S + (h + 1) * HALF],
+                    start=True, stop=False,
+                )
+                nc.tensor.matmul_mx(
+                    out=acc[:],
+                    lhsT=late[:, WB_W + 4 * i * P : WB_W + 4 * (i + 1) * P].bitcast(E5M2),
+                    lhsT_scale=planes[:, WB_S + i * P : WB_S + (i + 1) * P],
+                    rhs=codes[h][:].bitcast(E4M3), rhs_scale=scales[h][:],
+                    start=False, stop=True,
+                )
+                st = tile(f"staged{h}{i}", HALF, F32)
+                if h == 1 and i == 0:
+                    nc.vector.tensor_copy(st[:], acc[:])
+                else:
+                    nc.scalar.copy(st[:], acc[:])
+                staged.append(st)
+            nc.vector.tensor_copy(pages[0][:].indirect(slots), staged[0][:])
+            nc.scalar.activation(out=pages[1][:].indirect(slots), in_=staged[1][:], func=ACT.Copy)
+
+        for i in range(N // P):
+            nc.sync.dma_start(out[i * P : (i + 1) * P, :], pages[i][:])

@@ -36,7 +36,11 @@ def tile_list_oneforboth_tablegate_skip_scattered_kernel(
     nc = tc.nc
     with ExitStack() as ctx:
         sb = ctx.enter_context(tc.tile_pool(name="sb", bufs=1))
+        shared = ctx.enter_context(tc.tile_pool(name="shared", bufs=1))
         ps = ctx.enter_context(tc.psum_pool(name="ps", bufs=1))
+
+        def shared_tile(name, width, dtype, offset):
+            return shared.tile([P, width], dtype, name=name, align_bytes=64, offset=offset)
 
         def tile(name, width, dtype, tag=""):
             return sb.tile([P, width], dtype, name=name, tag=tag or name, align_bytes=64)
@@ -46,46 +50,48 @@ def tile_list_oneforboth_tablegate_skip_scattered_kernel(
             nc.sync.dma_start(dst[:], src)
             return dst
 
-        def load_words(dst, src):
-            nc.sync.dma_start(dst.bitcast(I32), src.bitcast(I32))
+        def load_words(dst, src, queue=nc.sync):
+            queue.dma_start(dst.bitcast(I32), src.bitcast(I32))
 
-        def load_scale_rows(dst, src):
-            nc.sync.dma_start(dst.bitcast(I32), src[0].bitcast(I32))
+        def load_scale_rows(queue, dst, src):
+            queue.dma_start(dst.bitcast(I32), src[0].bitcast(I32))
 
         xt_s_win = tile("xt_s_win", T, U8)
         xo_s_win = tile("xo_s_win", T, U8)
         w_s_raw = tile("w_s_raw", R, U8)
         rows = tile("rows", W_END, U8, tag="rows_then_words")
         planes = tile("planes", S_END, U8)
-        xt_win = tile("xt_win", T, U32)
-        xo_win = tile("xo_win", T, U16)
-        w_raw = tile("w_raw", R, I32)
-        pages = [tile(f"page{i}", E, F32) for i in range(N // P)]
+        xt_win = tile("xt_win", T, U32, tag="xt_then_page")
+        xo_win = shared_tile("xo_win", T, U16, 4096)
+        w_raw = shared_tile("w_raw", R, I32, 0)
+        page_b = tile("page_b", E, F32)
 
         list_xt = load_list("list_xt", offs)
         list_xo = load_list("list_xo", offs2)
-        for dst, src in ((xt_s_win, xt_scales), (xo_s_win, xo_scales), (w_s_raw, w_scales)):
+        for queue, dst, src in (
+            (nc.scalar, xt_s_win, xt_scales), (nc.scalar, xo_s_win, xo_scales), (nc.sync, w_s_raw, w_scales)
+        ):
             nc.vector.memset(dst[0:ROW0, :].bitcast(I32), 0)
-            load_scale_rows(dst[ROW0:P, :], src)
-        load_words(xo_win[:], xo_words[0])
+            load_scale_rows(queue, dst[ROW0:P, :], src)
+        load_scale_rows(nc.scalar, rows[ROW0:P, WB_S:WS_S], wb_scales)
         load_words(w_raw[:], w_words[0].rearrange("p c r -> p (c r)"))
-        load_words(xt_win[:], xt_words[0].rearrange("p c r -> p (c r)"))
-        for c0, src in ((WB_S, wb_scales), (WS_S, ws_scales), (SX_S, sx_scales)):
-            load_scale_rows(rows[ROW0:P, c0 : c0 + 256], src)
+        load_words(xt_win[:], xt_words[0].rearrange("p c r -> p (c r)"), nc.scalar)
+        load_scale_rows(nc.sync, rows[ROW0:P, WS_S:SX_S], ws_scales)
+        load_scale_rows(nc.sync, rows[ROW0:P, SX_S:S_END], sx_scales)
+        load_words(xo_win[:], xo_words[0])
         list_tg = load_list("list_tg", offs3)
-        list_out = load_list("list_out", offs4)
         slope = tile("slope", PACK, F32)
         shift = tile("shift", PACK, F32)
-        nc.gpsimd.dma_start(slope[:], sg.rearrange("(p t) o -> p (t o)", t=PACK))
-        nc.gpsimd.dma_start(shift[:], bg.rearrange("(p t) o -> p (t o)", t=PACK))
         tg_by_t = tg.rearrange("(p t) q -> p t q", t=PACK)
-        tg_win = [tile(f"tg_win{t}", T, F32) for t in range(PACK)]
-        for t in range(PACK):
-            nc.sync.dma_start(tg_win[t][:], tg_by_t[:, t, :])
+        tg_win = [tile(f"tg_win{t}", T, F32) for t in range(2)]
+        for dst, src in ((slope, sg), (shift, bg)):
+            nc.gpsimd.dma_start(dst[:], src.rearrange("(p t) o -> p (t o)", t=PACK))
+        nc.sync.dma_start(tg_win[0][:], tg_by_t[:, 0, :])
+        list_out = load_list("list_out", offs4)
+        nc.sync.dma_start(tg_win[1][:], tg_by_t[:, 1, :])
 
         nc.vector.memset(planes[:].bitcast(I32), 0)
-        for page in pages:
-            nc.vector.memset(page[:], 0.0)
+        nc.gpsimd.memset(page_b[:].bitcast(I32), 0)
 
         xt_s = tile("xt_s", J, U8)
         xo_s = tile("xo_s", J, U8)
@@ -103,55 +109,83 @@ def tile_list_oneforboth_tablegate_skip_scattered_kernel(
                 rows[ROW0 + 4 * q : ROW0 + 4 * q + 4, 0:S_END].bitcast(I32),
             )
 
-        late = tile("late", W_END, U8, tag="rows_then_words")
-        load_words(late[:, WS_W:SX_W], ws_words[0].rearrange("p c r -> p (c r)"))
-        load_words(late[:, SX_W:W_END], sx_words[0])
-        load_words(late[:, WB_W:WS_W], wb_words[0].rearrange("p c r -> p (c r)"))
 
         xo_g = tile("xo_g", J, U16)
         xt_g = tile("xt_g", J, U32)
         w_dealt = tile("w_dealt", R, I32)
-        nc.vector.tensor_copy(xo_g[:], xo_win[:].indirect(list_xo[:]))
         nc.vector.tensor_copy(
             w_dealt[:].rearrange("p (t c i) -> p c t i", t=PACK, i=4),
             w_raw[:].rearrange("p (c i t) -> p c t i", t=PACK, i=4),
         )
         nc.vector.tensor_copy(xt_g[:], xt_win[:].indirect(list_xt[:]))
+        nc.vector.tensor_copy(xo_g[:], xo_win[:].indirect(list_xo[:]))
+        for t in (2, 3):
+            tg_win.append(shared_tile(f"tg_win{t}", T, F32, 4096 * (t - 2)))
+            nc.sync.dma_start(tg_win[t][:], tg_by_t[:, t, :])
+        page_a = tile("page_a", E, F32, tag="xt_then_page")
+        nc.vector.memset(page_a[:].bitcast(I32), 0)
+        pages = [page_a, page_b]
+        late = tile("late", W_END, U8, tag="rows_then_words")
+        load_words(late[:, WS_W:SX_W], ws_words[0].rearrange("p c r -> p (c r)"))
+        load_words(late[:, SX_W:W_END], sx_words[0])
+        load_words(late[:, WB_W:WS_W], wb_words[0].rearrange("p c r -> p (c r)"))
 
-        hid = tile("hid", PACK * J, BF16)
+        gates = tile("gates", PACK * J, F32)
         for t in range(PACK):
-            gate = tile(f"gate{t}", J, F32)
             nc.scalar.activation(
-                out=gate[:], in_=tg_win[t][:].indirect(list_tg[:]), func=ACT.Sigmoid,
+                out=gates[:, t * J : (t + 1) * J], in_=tg_win[t][:].indirect(list_tg[:]), func=ACT.Sigmoid,
                 bias=shift[:, t : t + 1], scale=slope[:, t : t + 1],
             )
-            ab = ps.tile([P, 2, J], F32, name=f"ab{t}")
-            for side, (codes, c0) in enumerate(((xo_g[:].bitcast(E2M1), XO_S), (xt_g[:].bitcast(E4M3), XT_S))):
-                nc.tensor.matmul_mx(
-                    out=ab[:, side, :],
-                    lhsT=w_dealt[:, t * P : (t + 1) * P].bitcast(E5M2),
-                    lhsT_scale=planes[:, W_S + t * P : W_S + (t + 1) * P],
-                    rhs=codes, rhs_scale=planes[:, c0 : c0 + J],
-                    start=True, stop=True,
-                )
-            larger = tile(f"larger{t}", J, F32)
-            if t < PACK - 1:
-                first = tile(f"first{t}", J, F32)
-                nc.scalar.copy(first[:], ab[:, 0, :])
-                nc.vector.tensor_tensor(larger[:], ab[:, 1, :], first[:], ALU.max)
-            else:
-                nc.vector.tensor_reduce(larger[:], ab[:].rearrange("p s j -> p j s"), AXIS.X, ALU.max)
-            nc.vector.tensor_tensor(hid[:, t * J : (t + 1) * J], larger[:], gate[:], ALU.mult)
 
-        hid_by_t = hid[:].rearrange("p (t j) -> p t j", t=PACK)
-        codes, scales, woven = [], [], []
-        for h in range(2):
-            wv = tile(f"woven{h}", PACK * HALF, BF16)
-            nc.vector.tensor_copy(
-                wv[:].rearrange("p (c i t) -> p c t i", t=PACK, i=4),
-                hid_by_t[:, :, h * HALF : (h + 1) * HALF].rearrange("p t (c i) -> p c t i", i=4),
+        larger = []
+        woven = [tile(f"woven{h}", PACK * HALF, BF16) for h in range(2)]
+        gates_by_t = gates[:].rearrange("p (t j) -> p t j", t=PACK)
+
+        def gate_and_weave(h, ts):
+            nc.vector.tensor_tensor(
+                woven[h][:].rearrange("p (c i t) -> p c t i", t=PACK, i=4)[:, :, ts, :],
+                larger[h][:].rearrange("p (t c i) -> p c t i", t=PACK, i=4)[:, :, ts, :],
+                gates_by_t[:, :, h * HALF : (h + 1) * HALF].rearrange("p t (c i) -> p c t i", i=4)[:, :, ts, :],
+                ALU.mult,
             )
-            woven.append(wv)
+
+        for h in range(2):
+            cols = slice(h * HALF, (h + 1) * HALF)
+            banks = []
+            for name, moving, c0 in (("a", xt_g[:, cols].bitcast(E4M3), XT_S), ("b", xo_g[:, cols].bitcast(E2M1), XO_S)):
+                bank = ps.tile([P, PACK * HALF], F32, name=f"{name}{h}")
+                for t in range(PACK):
+                    nc.tensor.matmul_mx(
+                        out=bank[:, t * HALF : (t + 1) * HALF],
+                        lhsT=w_dealt[:, t * P : (t + 1) * P].bitcast(E5M2),
+                        lhsT_scale=planes[:, W_S + t * P : W_S + (t + 1) * P],
+                        rhs=moving, rhs_scale=planes[:, c0 + h * HALF : c0 + (h + 1) * HALF],
+                        start=True, stop=True,
+                    )
+                banks.append(bank)
+            a_sb = tile("a_sb0", PACK * HALF, F32) if h == 0 else shared_tile("a_sb1", PACK * HALF, F32, 2048)
+            nc.scalar.copy(a_sb[:], banks[0][:])
+            larger.append(tile(f"larger{h}", PACK * HALF, F32))
+            nc.vector.tensor_tensor(larger[h][:], banks[1][:], a_sb[:], ALU.max)
+            if h == 0:
+                gate_and_weave(0, slice(0, PACK - 1))
+        gate_and_weave(0, slice(PACK - 1, PACK))
+        gate_and_weave(1, slice(0, PACK))
+
+        accs = {}
+        for h in range(2):
+            for i in range(N // P):
+                accs[h, i] = ps.tile([P, HALF], F32, name=f"acc{h}{i}")
+                nc.tensor.matmul_mx(
+                    out=accs[h, i][:],
+                    lhsT=late[:, WS_W + 4 * i * P : WS_W + 4 * (i + 1) * P].bitcast(E5M2),
+                    lhsT_scale=planes[:, WS_S + i * P : WS_S + (i + 1) * P],
+                    rhs=late[:, SX_W + 2 * h * HALF : SX_W + 2 * (h + 1) * HALF].bitcast(E2M1),
+                    rhs_scale=planes[:, SX_S + h * HALF : SX_S + (h + 1) * HALF],
+                    start=True, stop=False,
+                )
+
+        codes, scales = [], []
         for h in range(2):
             codes.append(tile(f"hid_codes{h}", HALF, U32))
             scales.append(tile(f"hid_scales{h}", HALF, U8))
@@ -161,15 +195,7 @@ def tile_list_oneforboth_tablegate_skip_scattered_kernel(
             slots = list_out[:, h * HALF // 16 : (h + 1) * HALF // 16]
             staged = []
             for i in range(N // P):
-                acc = ps.tile([P, HALF], F32, name=f"acc{h}{i}")
-                nc.tensor.matmul_mx(
-                    out=acc[:],
-                    lhsT=late[:, WS_W + 4 * i * P : WS_W + 4 * (i + 1) * P].bitcast(E5M2),
-                    lhsT_scale=planes[:, WS_S + i * P : WS_S + (i + 1) * P],
-                    rhs=late[:, SX_W + 2 * h * HALF : SX_W + 2 * (h + 1) * HALF].bitcast(E2M1),
-                    rhs_scale=planes[:, SX_S + h * HALF : SX_S + (h + 1) * HALF],
-                    start=True, stop=False,
-                )
+                acc = accs[h, i]
                 nc.tensor.matmul_mx(
                     out=acc[:],
                     lhsT=late[:, WB_W + 4 * i * P : WB_W + 4 * (i + 1) * P].bitcast(E5M2),
@@ -186,5 +212,5 @@ def tile_list_oneforboth_tablegate_skip_scattered_kernel(
             nc.vector.tensor_copy(pages[0][:].indirect(slots), staged[0][:])
             nc.scalar.activation(out=pages[1][:].indirect(slots), in_=staged[1][:], func=ACT.Copy)
 
-        for i in range(N // P):
-            nc.sync.dma_start(out[i * P : (i + 1) * P, :], pages[i][:])
+        for i, queue in enumerate((nc.sync, nc.scalar)):
+            queue.dma_start(out[i * P : (i + 1) * P, :], pages[i][:])

@@ -62,8 +62,7 @@ def tile_list_oneforboth_tablegate_skip_scattered_kernel(
         rows = tile("rows", W_END, U8, tag="rows_then_words")
         planes = tile("planes", S_END, U8)
         xt_win = tile("xt_win", T, U32, tag="xt_then_page")
-        xo_win = shared_tile("xo_win", T, U16, 4096)
-        w_raw = shared_tile("w_raw", R, I32, 0)
+        w_raw = tile("w_raw", R, I32)
         page_b = tile("page_b", E, F32)
 
         list_xt = load_list("list_xt", offs)
@@ -78,7 +77,6 @@ def tile_list_oneforboth_tablegate_skip_scattered_kernel(
         load_words(xt_win[:], xt_words[0].rearrange("p c r -> p (c r)"), nc.scalar)
         load_scale_rows(nc.sync, rows[ROW0:P, WS_S:SX_S], ws_scales)
         load_scale_rows(nc.sync, rows[ROW0:P, SX_S:S_END], sx_scales)
-        load_words(xo_win[:], xo_words[0])
         list_tg = load_list("list_tg", offs3)
         slope = tile("slope", PACK, F32)
         shift = tile("shift", PACK, F32)
@@ -94,37 +92,42 @@ def tile_list_oneforboth_tablegate_skip_scattered_kernel(
         nc.gpsimd.memset(page_b[:].bitcast(I32), 0)
 
         xt_s = tile("xt_s", J, U8)
-        xo_s = tile("xo_s", J, U8)
+        xo_s = shared_tile("xo_s", 4096 + J, U8, 4096 - 128)[:, 0:J]
         nc.vector.tensor_copy(xt_s[:], xt_s_win[:].indirect(list_xt[:]))
-        nc.vector.tensor_copy(xo_s[:], xo_s_win[:].indirect(list_xo[:]))
+        nc.vector.tensor_copy(xo_s, xo_s_win[:].indirect(list_xo[:]))
         nc.vector.tensor_copy(
             rows[:, W_S:WB_S].rearrange("p (t c i) -> p c t i", t=PACK, i=16),
             w_s_raw[:].rearrange("p (c i t) -> p c t i", t=PACK, i=16),
         )
         nc.vector.tensor_copy(rows[:, XT_S:XO_S].bitcast(I32), xt_s[:].bitcast(I32))
-        nc.vector.tensor_copy(rows[:, XO_S:W_S].bitcast(I32), xo_s[:].bitcast(I32))
+        nc.vector.tensor_copy(rows[:, XO_S:W_S].bitcast(I32), xo_s.bitcast(I32))
         for q in range(4):
-            nc.scalar.dma_start(
+            nc.sync.dma_start(
                 planes[32 * q : 32 * q + 4, :].bitcast(I32),
                 rows[ROW0 + 4 * q : ROW0 + 4 * q + 4, 0:S_END].bitcast(I32),
             )
-
+        xo_win = shared_tile("xo_win", T, U16, 4096)
+        load_words(xo_win[:], xo_words[0])
+        for t, offset in ((2, 0), (3, 8192)):
+            tg_win.append(shared_tile(f"tg_win{t}", T, F32, offset))
+            nc.sync.dma_start(tg_win[t][:], tg_by_t[:, t, :])
 
         xo_g = tile("xo_g", J, U16)
         xt_g = tile("xt_g", J, U32)
-        w_dealt = tile("w_dealt", R, I32)
+        w_dealt = shared_tile("w_dealt", R, I32, 6144)
         nc.vector.tensor_copy(
             w_dealt[:].rearrange("p (t c i) -> p c t i", t=PACK, i=4),
             w_raw[:].rearrange("p (c i t) -> p c t i", t=PACK, i=4),
         )
         nc.vector.tensor_copy(xt_g[:], xt_win[:].indirect(list_xt[:]))
-        nc.vector.tensor_copy(xo_g[:], xo_win[:].indirect(list_xo[:]))
-        for t in (2, 3):
-            tg_win.append(shared_tile(f"tg_win{t}", T, F32, 4096 * (t - 2)))
-            nc.sync.dma_start(tg_win[t][:], tg_by_t[:, t, :])
         page_a = tile("page_a", E, F32, tag="xt_then_page")
         nc.vector.memset(page_a[:].bitcast(I32), 0)
         pages = [page_a, page_b]
+        for h in range(2):
+            nc.vector.tensor_copy(
+                xo_g[:, h * HALF : (h + 1) * HALF],
+                xo_win[:].indirect(list_xo[:, h * HALF // 16 : (h + 1) * HALF // 16]),
+            )
         late = tile("late", W_END, U8, tag="rows_then_words")
         load_words(late[:, WS_W:SX_W], ws_words[0].rearrange("p c r -> p (c r)"))
         load_words(late[:, SX_W:W_END], sx_words[0])
@@ -138,6 +141,7 @@ def tile_list_oneforboth_tablegate_skip_scattered_kernel(
             )
 
         larger = []
+        early, last = slice(0, PACK - 1), slice(PACK - 1, PACK)
         woven = [tile(f"woven{h}", PACK * HALF, BF16) for h in range(2)]
         gates_by_t = gates[:].rearrange("p (t j) -> p t j", t=PACK)
 
@@ -163,14 +167,12 @@ def tile_list_oneforboth_tablegate_skip_scattered_kernel(
                         start=True, stop=True,
                     )
                 banks.append(bank)
-            a_sb = tile("a_sb0", PACK * HALF, F32) if h == 0 else shared_tile("a_sb1", PACK * HALF, F32, 2048)
+            a_sb = tile("a_sb0", PACK * HALF, F32) if h == 0 else shared_tile("a_sb1", PACK * HALF, F32, 0)
             nc.scalar.copy(a_sb[:], banks[0][:])
             larger.append(tile(f"larger{h}", PACK * HALF, F32))
             nc.vector.tensor_tensor(larger[h][:], banks[1][:], a_sb[:], ALU.max)
             if h == 0:
-                gate_and_weave(0, slice(0, PACK - 1))
-        gate_and_weave(0, slice(PACK - 1, PACK))
-        gate_and_weave(1, slice(0, PACK))
+                gate_and_weave(0, early)
 
         accs = {}
         for h in range(2):
@@ -189,6 +191,9 @@ def tile_list_oneforboth_tablegate_skip_scattered_kernel(
         for h in range(2):
             codes.append(tile(f"hid_codes{h}", HALF, U32))
             scales.append(tile(f"hid_scales{h}", HALF, U8))
+            gate_and_weave(h, last)
+            if h == 0:
+                gate_and_weave(1, early)
             nc.vector.quantize_mx(out=codes[h][:].bitcast(E4M3), scales=scales[h][:], in_=woven[h][:])
 
         for h in range(2):
@@ -204,10 +209,7 @@ def tile_list_oneforboth_tablegate_skip_scattered_kernel(
                     start=False, stop=True,
                 )
                 st = tile(f"staged{h}{i}", HALF, F32)
-                if h == 1 and i == 0:
-                    nc.vector.tensor_copy(st[:], acc[:])
-                else:
-                    nc.scalar.copy(st[:], acc[:])
+                nc.scalar.copy(st[:], acc[:])
                 staged.append(st)
             nc.vector.tensor_copy(pages[0][:].indirect(slots), staged[0][:])
             nc.scalar.activation(out=pages[1][:].indirect(slots), in_=staged[1][:], func=ACT.Copy)

@@ -77,6 +77,9 @@ def tile_list_oneforboth_tablegate_skip_scattered_kernel(
         load_words(xt_win[:], xt_words[0].rearrange("p c r -> p (c r)"), nc.scalar)
         load_scale_rows(nc.sync, rows[ROW0:P, WS_S:SX_S], ws_scales)
         load_scale_rows(nc.sync, rows[ROW0:P, SX_S:S_END], sx_scales)
+        warm = tile("warm", 2, F32)
+        nc.vector.memset(warm[:, 0:1], 0.0)
+        nc.scalar.activation(out=warm[:, 1:2], in_=warm[:, 0:1], func=ACT.Sigmoid)
         list_tg = load_list("list_tg", offs3)
         slope = tile("slope", PACK, F32)
         shift = tile("shift", PACK, F32)

from contextlib import ExitStack

import concourse.mybir as mybir

K, T, J, R, N, E = 512, 1024, 256, 512, 256, 1024
FLOPS = 2 * J * (2 * K * R + 2 * R * N)

F32 = mybir.dt.float32
BF16 = mybir.dt.bfloat16
I32 = mybir.dt.int32
U32 = mybir.dt.uint32
U16 = mybir.dt.uint16
U8 = mybir.dt.uint8
E4M3 = mybir.dt.float8_e4m3fn_x4
E5M2 = mybir.dt.float8_e5m2_x4
E2M1 = mybir.dt.float4_e2m1fn_x4
ALU = mybir.AluOpType
ACT = mybir.ActivationFunctionType
AXIS = mybir.AxisListType

P = 128
PACK = 4
ROWS = 16
ROW0 = P - ROWS
HALF = J // 2

XT_S, XO_S, W_S, WB_S, WS_S, SX_S, S_END = 0, 256, 512, 1024, 1280, 1536, 1792
WB_W, WS_W, SX_W, W_END = 0, 1024, 2048, 2560


def tile_list_oneforboth_tablegate_skip_scattered_kernel(
    tc, xt_words, xt_scales, xo_words, xo_scales, w_words, w_scales, tg, sg, bg,
    wb_words, wb_scales, sx_words, sx_scales, ws_words, ws_scales,
    offs, offs2, offs3, offs4, out,
):
    nc = tc.nc
    with ExitStack() as ctx:
        sb = ctx.enter_context(tc.tile_pool(name="sb", bufs=1))
        shared = ctx.enter_context(tc.tile_pool(name="shared", bufs=1))
        ps = ctx.enter_context(tc.psum_pool(name="ps", bufs=1))

        def shared_tile(name, width, dtype, offset):
            return shared.tile([P, width], dtype, name=name, align_bytes=64, offset=offset)

        def tile(name, width, dtype, tag=""):
            return sb.tile([P, width], dtype, name=name, tag=tag or name, align_bytes=64)

        def load_list(name, src):
            dst = sb.tile([P, J // 16], U16, name=name)
            nc.sync.dma_start(dst[:], src)
            return dst

        def load_words(dst, src, queue=nc.sync):
            queue.dma_start(dst.bitcast(I32), src.bitcast(I32))

        def load_scale_rows(queue, dst, src):
            queue.dma_start(dst.bitcast(I32), src[0].bitcast(I32))

        xt_s_win = tile("xt_s_win", T, U8)
        xo_s_win = tile("xo_s_win", T, U8)
        w_s_raw = tile("w_s_raw", R, U8)
        rows = tile("rows", W_END, U8, tag="rows_then_words")
        planes = tile("planes", S_END, U8)
        xt_win = tile("xt_win", T, U32, tag="xt_then_page")
        w_raw = tile("w_raw", R, I32)
        page_b = tile("page_b", E, F32)

        list_xt = load_list("list_xt", offs)
        list_xo = load_list("list_xo", offs2)
        for queue, dst, src in (
            (nc.scalar, xt_s_win, xt_scales), (nc.scalar, xo_s_win, xo_scales), (nc.sync, w_s_raw, w_scales)
        ):
            nc.vector.memset(dst[0:ROW0, :].bitcast(I32), 0)
            load_scale_rows(queue, dst[ROW0:P, :], src)
        load_scale_rows(nc.scalar, rows[ROW0:P, WB_S:WS_S], wb_scales)
        load_words(w_raw[:], w_words[0].rearrange("p c r -> p (c r)"))
        load_words(xt_win[:], xt_words[0].rearrange("p c r -> p (c r)"), nc.scalar)
        load_scale_rows(nc.sync, rows[ROW0:P, WS_S:SX_S], ws_scales)
        load_scale_rows(nc.sync, rows[ROW0:P, SX_S:S_END], sx_scales)
        warm = tile("warm", 2, F32)
        nc.vector.memset(warm[:, 0:1], 0.0)
        nc.scalar.activation(out=warm[:, 1:2], in_=warm[:, 0:1], func=ACT.Sigmoid)
        list_tg = load_list("list_tg", offs3)
        slope = tile("slope", PACK, F32)
        shift = tile("shift", PACK, F32)
        tg_by_t = tg.rearrange("(p t) q -> p t q", t=PACK)
        tg_win = [tile(f"tg_win{t}", T, F32) for t in range(2)]
        for dst, src in ((slope, sg), (shift, bg)):
            nc.gpsimd.dma_start(dst[:], src.rearrange("(p t) o -> p (t o)", t=PACK))
        nc.sync.dma_start(tg_win[0][:], tg_by_t[:, 0, :])
        list_out = load_list("list_out", offs4)
        nc.sync.dma_start(tg_win[1][:], tg_by_t[:, 1, :])

        nc.vector.memset(planes[:].bitcast(I32), 0)
        nc.gpsimd.memset(page_b[:].bitcast(I32), 0)

        xt_s = tile("xt_s", J, U8)
        xo_s = shared_tile("xo_s", 4096 + J, U8, 4096 - 128)[:, 0:J]
        nc.vector.tensor_copy(xt_s[:], xt_s_win[:].indirect(list_xt[:]))
        nc.vector.tensor_copy(xo_s, xo_s_win[:].indirect(list_xo[:]))
        nc.vector.tensor_copy(
            rows[:, W_S:WB_S].rearrange("p (t c i) -> p c t i", t=PACK, i=16),
            w_s_raw[:].rearrange("p (c i t) -> p c t i", t=PACK, i=16),
        )
        nc.vector.tensor_copy(rows[:, XT_S:XO_S].bitcast(I32), xt_s[:].bitcast(I32))
        nc.vector.tensor_copy(rows[:, XO_S:W_S].bitcast(I32), xo_s.bitcast(I32))
        for q in range(4):
            nc.sync.dma_start(
                planes[32 * q : 32 * q + 4, :].bitcast(I32),
                rows[ROW0 + 4 * q : ROW0 + 4 * q + 4, 0:S_END].bitcast(I32),
            )
        xo_win = shared_tile("xo_win", T, U16, 4096)
        load_words(xo_win[:], xo_words[0])
        for t, offset in ((2, 0), (3, 8192)):
            tg_win.append(shared_tile(f"tg_win{t}", T, F32, offset))
            nc.sync.dma_start(tg_win[t][:], tg_by_t[:, t, :])

        xo_g = tile("xo_g", J, U16)
        xt_g = tile("xt_g", J, U32)
        w_dealt = shared_tile("w_dealt", R, I32, 6144)
        nc.vector.tensor_copy(
            w_dealt[:].rearrange("p (t c i) -> p c t i", t=PACK, i=4),
            w_raw[:].rearrange("p (c i t) -> p c t i", t=PACK, i=4),
        )
        nc.vector.tensor_copy(xt_g[:], xt_win[:].indirect(list_xt[:]))
        page_a = tile("page_a", E, F32, tag="xt_then_page")
        nc.vector.memset(page_a[:].bitcast(I32), 0)
        pages = [page_a, page_b]
        for h in range(2):
            nc.vector.tensor_copy(
                xo_g[:, h * HALF : (h + 1) * HALF],
                xo_win[:].indirect(list_xo[:, h * HALF // 16 : (h + 1) * HALF // 16]),
            )
        late = tile("late", W_END, U8, tag="rows_then_words")
        load_words(late[:, WS_W:SX_W], ws_words[0].rearrange("p c r -> p (c r)"))
        load_words(late[:, SX_W:W_END], sx_words[0])
        load_words(late[:, WB_W:WS_W], wb_words[0].rearrange("p c r -> p (c r)"))

        gates = tile("gates", PACK * J, F32)
        for t in range(PACK):
            nc.scalar.activation(
                out=gates[:, t * J : (t + 1) * J], in_=tg_win[t][:].indirect(list_tg[:]), func=ACT.Sigmoid,
                bias=shift[:, t : t + 1], scale=slope[:, t : t + 1],
            )

        larger = []
        early, last = slice(0, PACK - 1), slice(PACK - 1, PACK)
        woven = [tile(f"woven{h}", PACK * HALF, BF16) for h in range(2)]
        gates_by_t = gates[:].rearrange("p (t j) -> p t j", t=PACK)

        def gate_and_weave(h, ts):
            nc.vector.tensor_tensor(
                woven[h][:].rearrange("p (c i t) -> p c t i", t=PACK, i=4)[:, :, ts, :],
                larger[h][:].rearrange("p (t c i) -> p c t i", t=PACK, i=4)[:, :, ts, :],
                gates_by_t[:, :, h * HALF : (h + 1) * HALF].rearrange("p t (c i) -> p c t i", i=4)[:, :, ts, :],
                ALU.mult,
            )

        for h in range(2):
            cols = slice(h * HALF, (h + 1) * HALF)
            banks = []
            for name, moving, c0 in (("a", xt_g[:, cols].bitcast(E4M3), XT_S), ("b", xo_g[:, cols].bitcast(E2M1), XO_S)):
                bank = ps.tile([P, PACK * HALF], F32, name=f"{name}{h}")
                for t in range(PACK):
                    nc.tensor.matmul_mx(
                        out=bank[:, t * HALF : (t + 1) * HALF],
                        lhsT=w_dealt[:, t * P : (t + 1) * P].bitcast(E5M2),
                        lhsT_scale=planes[:, W_S + t * P : W_S + (t + 1) * P],
                        rhs=moving, rhs_scale=planes[:, c0 + h * HALF : c0 + (h + 1) * HALF],
                        start=True, stop=True,
                    )
                banks.append(bank)
            a_sb = tile("a_sb0", PACK * HALF, F32) if h == 0 else shared_tile("a_sb1", PACK * HALF, F32, 0)
            nc.scalar.copy(a_sb[:], banks[0][:])
            larger.append(tile(f"larger{h}", PACK * HALF, F32))
            nc.vector.tensor_tensor(larger[h][:], banks[1][:], a_sb[:], ALU.max)
            if h == 0:
                gate_and_weave(0, early)

        accs = {}
        for h in range(2):
            for i in range(N // P):
                accs[h, i] = ps.tile([P, HALF], F32, name=f"acc{h}{i}")
                nc.tensor.matmul_mx(
                    out=accs[h, i][:],
                    lhsT=late[:, WS_W + 4 * i * P : WS_W + 4 * (i + 1) * P].bitcast(E5M2),
                    lhsT_scale=planes[:, WS_S + i * P : WS_S + (i + 1) * P],
                    rhs=late[:, SX_W + 2 * h * HALF : SX_W + 2 * (h + 1) * HALF].bitcast(E2M1),
                    rhs_scale=planes[:, SX_S + h * HALF : SX_S + (h + 1) * HALF],
                    start=True, stop=False,
                )

        codes, scales = [], []
        for h in range(2):
            codes.append(tile(f"hid_codes{h}", HALF, U32))
            scales.append(tile(f"hid_scales{h}", HALF, U8))
            gate_and_weave(h, last)
            if h == 0:
                gate_and_weave(1, early)
            nc.vector.quantize_mx(out=codes[h][:].bitcast(E4M3), scales=scales[h][:], in_=woven[h][:])

        for h in range(2):
            slots = list_out[:, h * HALF // 16 : (h + 1) * HALF // 16]
            staged = []
            for i in range(N // P):
                acc = accs[h, i]
                nc.tensor.matmul_mx(
                    out=acc[:],
                    lhsT=late[:, WB_W + 4 * i * P : WB_W + 4 * (i + 1) * P].bitcast(E5M2),
                    lhsT_scale=planes[:, WB_S + i * P : WB_S + (i + 1) * P],
                    rhs=codes[h][:].bitcast(E4M3), rhs_scale=scales[h][:],
                    start=False, stop=True,
                )
                st = tile(f"staged{h}{i}", HALF, F32)
                nc.scalar.copy(st[:], acc[:])
                staged.append(st)
            nc.vector.tensor_copy(pages[0][:].indirect(slots), staged[0][:])
            nc.scalar.activation(out=pages[1][:].indirect(slots), in_=staged[1][:], func=ACT.Copy)

        for i, queue in enumerate((nc.sync, nc.scalar)):
            queue.dma_start(out[i * P : (i + 1) * P, :], pages[i][:])
